import numpy as np
import ml_dtypes


def mxq(x, axis, fmt="e4m3"):
    dtype, down = {"e4m3": (ml_dtypes.float8_e4m3fn, 7), "e5m2": (ml_dtypes.float8_e5m2, 14)}[fmt]
    v = np.moveaxis(np.asarray(x, np.float32).astype(ml_dtypes.bfloat16).astype(np.float64), axis, -1)
    blocks = v.reshape(v.shape[:-1] + (-1, 32))
    amax = np.abs(blocks).max(-1, keepdims=True)
    byte = np.maximum(np.where(amax > 0, np.frexp(amax)[1] - 1 + 127, 0) - down, 1)
    scale = np.exp2(byte - 127.0)
    codes = (blocks / scale).astype(np.float32).astype(dtype).astype(np.float64)
    return np.moveaxis((codes * scale).reshape(v.shape), -1, axis)


WIDE = False


def mx_kscale(k):
    if not WIDE:
        return np.ones(k)
    levels = np.array([10, -10, 5, -5, 0])
    if k % 512:
        return np.exp2(np.random.permutation(np.resize(levels, k // 32))).repeat(32)
    a = np.empty((k // 512, 16))
    for p in range(k // 512):
        a[p, :8] = np.random.permutation(np.resize(levels, 8))
        for g in range(8):
            far = levels[np.abs(levels - a[p, g]) >= 10]
            a[p, g + 8] = far[np.random.randint(len(far))]
    return np.exp2(a.ravel()).repeat(32)


def f64(x):
    return np.asarray(x).astype(np.float64)


def striped(idx):
    return np.tile(idx.reshape(-1, 16).T, (8, 1)).astype(np.uint16)


def unstriped(offs):
    return offs[:16].T.reshape(-1).astype(np.int64)


def striped8(idx):
    return np.concatenate([x.reshape(-1, 16).T for x in idx]).astype(np.uint16)


def runs(offs, k):
    lists = np.stack([offs[16 * r : 16 * r + 16].T.reshape(-1) for r in range(8)]).astype(np.int64)
    return lists[np.arange(k) % 512 // 64]


def pack_weight(w):
    k, n = w.shape
    w = f64(np.asarray(w, np.float32).astype(ml_dtypes.bfloat16)).reshape(k // 32, 32, n)
    amax = np.abs(w).max(1)
    byte = np.clip(np.where(amax > 0, np.frexp(amax)[1] - 1 + 127 - 7, 1), 1, 254)
    scaled = (w * np.exp2(127.0 - byte)[:, None, :]).reshape(k, n).astype(np.float32)
    words = np.ascontiguousarray(scaled.reshape(k // 512, 128, 4, n).transpose(0, 1, 3, 2)).astype(ml_dtypes.float8_e4m3fn).view(np.uint8)
    return words, np.ascontiguousarray(byte.astype(np.uint8).reshape(k // 512, 16, n))


def unpack_weight(words, scales):
    g, p, n, _ = words.shape
    vals = np.ascontiguousarray(words).view(ml_dtypes.float8_e4m3fn).astype(np.float64) * np.repeat(np.exp2(scales.astype(np.float64) - 127.0), 8, axis=1)[..., None]
    return vals.transpose(0, 1, 3, 2).reshape(g * 512, n)

def planes(y):
    n, m = y.shape
    v = y.astype(np.float32).astype(ml_dtypes.bfloat16).astype(np.float64).reshape(n // 32, 32, m)
    top = np.abs(v).max(1)
    byte = np.clip(np.where(top > 0, np.frexp(top)[1] - 1 + 127 - 7, 1), 1, 254)
    codes = (v * np.exp2(127.0 - byte)[:, None, :]).reshape(n, m).astype(np.float32).astype(ml_dtypes.float8_e4m3fn).view(np.uint8)
    words = codes.reshape(n // 512, 128, 4, m).transpose(0, 1, 3, 2)
    return np.ascontiguousarray(words), np.ascontiguousarray(byte.astype(np.uint8).reshape(n // 512, 16, m))


K, T, S, N, H, W = 512, 2048, 512, 512, 512, 256


def setup_inputs():
    n = np.random.standard_normal
    s = mx_kscale(K)[:, None]
    u = mx_kscale(H)
    packed_xT = pack_weight(n((K, T)) * s)
    packed_w1 = pack_weight(n((K, H)) / np.sqrt(K) / s)
    packed_w2 = pack_weight(n((K, H)) / np.sqrt(K) / s)
    packed_w3 = pack_weight(n((K, H)) / np.sqrt(K) / s)
    packed_w4 = pack_weight(n((H, N)) / np.sqrt(H) / u[:, None])
    return {
        "x_words": packed_xT[0],
        "x_scales": packed_xT[1],
        "w1_words": packed_w1[0],
        "w1_scales": packed_w1[1],
        "w2_words": packed_w2[0],
        "w2_scales": packed_w2[1],
        "w3_words": packed_w3[0],
        "w3_scales": packed_w3[1],
        "gn": (np.random.uniform(0.5, 1.5, (H, 1)) * u[:, None]).astype(np.float32),
        "w4_words": packed_w4[0],
        "w4_scales": packed_w4[1],
        "offs": striped(np.random.permutation(T)[:S]),
        "two": striped(np.random.permutation(T)[:S]),
        "three": striped(np.random.permutation(T)[:S]),
        "n1": striped8(np.stack([np.random.permutation(S)[:W] for _ in range(8)])),
        "n2": striped8(np.stack([np.random.permutation(S)[:W] for _ in range(8)])),
        "n3": striped8(np.stack([np.random.permutation(S) for _ in range(8)])),
        "n4": striped8(np.stack([np.random.permutation(S) for _ in range(8)])),
        "n5": striped8(np.stack([np.random.permutation(S) for _ in range(8)])),
        "n6": striped8(np.stack([np.random.permutation(S) for _ in range(8)])),
        "n7": striped8(np.stack([np.random.permutation(S) for _ in range(8)])),
    }


def reference(x_words, x_scales, w1_words, w1_scales, w2_words, w2_scales, w3_words, w3_scales, gn, w4_words, w4_scales, offs, two, three, n1, n2, n3, n4, n5, n6, n7):
    x_two = unpack_weight(x_words, x_scales)[:, unstriped(two)]
    d = unpack_weight(w2_words, w2_scales).T @ x_two
    xq = unpack_weight(x_words, x_scales)[:, unstriped(offs)]
    y = unpack_weight(w1_words, w1_scales).T @ xq
    ra = d[np.arange(H)[:, None], runs(n2, H)] - (0.5 * (y[np.arange(H)[:, None], runs(n1, H)]))
    m1 = y.copy()
    m1[np.arange(H)[:, None], runs(n1, H)] = ra
    x_three = unpack_weight(x_words, x_scales)[:, unstriped(three)]
    b = unpack_weight(w3_words, w3_scales).T @ x_three
    z = f64(gn) * ((m1 - (m1[np.arange(H)[:, None], runs(n3, H)])) / (np.abs(b) + np.abs(b[np.arange(H)[:, None], runs(n4, H)]) + 0.5))
    h = unpack_weight(w4_words, w4_scales).T @ mxq(z, 0, "e4m3")
    out_0 = h + h[np.arange(N)[:, None], runs(n5, N)] - (np.maximum(h[np.arange(N)[:, None], runs(n6, N)], h[np.arange(N)[:, None], runs(n7, N)]))
    return (out_0,) + planes(out_0)

@@ -1,0 +1,222 @@
+from contextlib import ExitStack
+
+import concourse.mybir as mybir
+
+K, T, S, H, N, W = 512, 2048, 512, 512, 512, 256
+P = 128
+PACK = 4
+FLOPS = 4 * 2 * K * H * S
+
+F32 = mybir.dt.float32
+BF16 = mybir.dt.bfloat16
+I32 = mybir.dt.int32
+U32 = mybir.dt.uint32
+U16 = mybir.dt.uint16
+U8 = mybir.dt.uint8
+FP8X4 = mybir.dt.float8_e4m3fn_x4
+ALU = mybir.AluOpType
+ACT = mybir.ActivationFunctionType
+
+Z_CHUNKS = ((0, 256), (256, 512))
+OUT_CHUNKS = ((0, 256), (256, 384), (384, 512))
+
+
+def tile_picked_trioputbnormbtrim_none_po_kernel(
+    tc, x_words, x_scales, w1_words, w1_scales, w2_words, w2_scales, w3_words, w3_scales, gn,
+    w4_words, w4_scales, offs, two, three, n1, n2, n3, n4, n5, n6, n7, out_0, out_1, out_2,
+):
+    nc = tc.nc
+    with ExitStack() as ctx:
+        lists = ctx.enter_context(tc.tile_pool(name="lists", bufs=1))
+        sb = ctx.enter_context(tc.tile_pool(name="sb", bufs=1))
+        psum = ctx.enter_context(tc.psum_pool(name="psum", bufs=1))
+
+        def tile(shape, dtype, name):
+            return sb.tile(shape, dtype, name=name, align_bytes=64)
+
+        def bank(index, width):
+            return psum.tile([P, width], F32, name=f"bank{index}")
+
+        def load_list(src, name):
+            dst = lists.tile(list(src.shape), U16, name=name)
+            nc.sync.dma_start(dst[:], src)
+            return dst
+
+        def load_words(src, name):
+            dst = tile([P, src.shape[2]], I32, name)
+            nc.sync.dma_start(dst[:], src[0].rearrange("p n t -> p (n t)").bitcast(I32))
+            return dst
+
+        def load_scales(queue, dst, first, src):
+            for q in range(4):
+                queue.dma_start(
+                    dst[32 * q + first : 32 * q + first + 4, :].bitcast(I32),
+                    src[0, 4 * q : 4 * q + 4, :].bitcast(I32),
+                )
+
+        xs = tile([P, T], U8, "xs")
+        ws31 = tile([P, H], U8, "ws31")
+        ws24 = tile([P, H], U8, "ws24")
+        nc.vector.memset(xs[:].bitcast(I32), 0)
+        nc.vector.memset(ws31[:].bitcast(I32), 0)
+        nc.gpsimd.memset(ws24[:].bitcast(I32), 0)
+
+        xw = load_words(x_words, "xw")
+        l_three = load_list(three, "three")
+        load_scales(nc.scalar, xs, 0, x_scales)
+        l_offs = load_list(offs, "offs")
+        w3raw = load_words(w3_words, "w3raw")
+        load_scales(nc.sync, ws31, 0, w3_scales)
+        load_scales(nc.sync, ws31, 4, w1_scales)
+        load_scales(nc.gpsimd, ws24, 4, w4_scales)
+        gain = tile([P, PACK], F32, "gain")
+        nc.gpsimd.dma_start(gain[:], gn.rearrange("(p t) o -> p (t o)", t=PACK))
+        w1raw = load_words(w1_words, "w1raw")
+        l_two = load_list(two, "two")
+        l4 = load_list(n4, "n4")
+        load_scales(nc.sync, ws24, 0, w2_scales)
+        w2raw = load_words(w2_words, "w2raw")
+        l1 = load_list(n1, "n1")
+        l2 = load_list(n2, "n2")
+        l3 = load_list(n3, "n3")
+        w4raw = load_words(w4_words, "w4raw")
+        l6 = load_list(n6, "n6")
+        l7 = load_list(n7, "n7")
+        l5 = load_list(n5, "n5")
+
+        neg_gain = tile([P, PACK], F32, "neg_gain")
+        nc.gpsimd.tensor_scalar(neg_gain[:], gain[:], -1.0, 0.0, ALU.mult, ALU.add)
+
+        def deal(raw, dtype, name):
+            dealt = tile([P, H], dtype, name)
+            nc.vector.tensor_copy(
+                dealt[:].rearrange("p (t c i) -> p c t i", t=PACK, i=4),
+                raw[:].rearrange("p (c i t) -> p c t i", t=PACK, i=4),
+            )
+            return dealt
+
+        def pick_words(lst, name):
+            dst = tile([P, S], U32, name)
+            nc.vector.tensor_copy(dst[:], xw[:].bitcast(U32).indirect(lst[:]))
+            return dst
+
+        def pick_scales(lst, name):
+            dst = tile([P, S], U8, name)
+            nc.vector.tensor_copy(dst[:], xs[:].indirect(lst[:]))
+            return dst
+
+        def product(acc, t, w, w_scale, first, words, scale):
+            cols = slice(P * t, P * (t + 1))
+            nc.tensor.matmul_mx(
+                out=acc, lhsT=w[:, cols].bitcast(FP8X4), lhsT_scale=w_scale[first:P, cols],
+                rhs=words.bitcast(FP8X4), rhs_scale=scale, start=True, stop=True,
+            )
+
+        x3w = pick_words(l_three, "x3w")
+        x3s = pick_scales(l_three, "x3s")
+        w3 = deal(w3raw, I32, "w3")
+        s31 = deal(ws31, U8, "s31")
+        x1w = pick_words(l_offs, "x1w")
+        x1s = pick_scales(l_offs, "x1s")
+        w1 = deal(w1raw, I32, "w1")
+        x2w = pick_words(l_two, "x2w")
+        x2s = pick_scales(l_two, "x2s")
+        w2 = deal(w2raw, I32, "w2")
+        s24 = deal(ws24, U8, "s24")
+
+        size_win = [tile([P, 2 * S], F32, f"size_win{t}") for t in range(PACK)]
+        size = tile([P, PACK, S], F32, "size")
+        for t in range(PACK):
+            acc = bank(t, S)
+            product(acc[:], t, w3, s31, 0, x3w[:], x3s[:])
+            nc.scalar.activation(size_win[t][:, :S], acc[:], ACT.Abs)
+            nc.scalar.activation(size[:, t, :], acc[:], ACT.Abs)
+
+        m_win = [tile([P, 2 * S], F32, f"m_win{t}") for t in range(PACK)]
+        for t in range(PACK):
+            acc = bank(4 + t, S)
+            product(acc[:], t, w1, s31, 4, x1w[:], x1s[:])
+            nc.scalar.activation(m_win[t][:, :S], acc[:], ACT.Copy, scale=neg_gain[:, t : t + 1])
+
+        d_win = [tile([P, S], F32, f"d_win{t}") for t in range(PACK)]
+        for t in range(PACK):
+            acc = bank(t, S)
+            product(acc[:], t, w2, s24, 0, x2w[:], x2s[:])
+            nc.scalar.activation(d_win[t][:], acc[:], ACT.Copy, scale=neg_gain[:, t : t + 1])
+
+        den = tile([P, PACK, S], F32, "den")
+        for t in range(PACK):
+            nc.vector.tensor_tensor(den[:, t, :], size_win[t][:].indirect(l4[:]), size[:, t, :], ALU.add)
+        log_den = tile([P, PACK, S], F32, "log_den")
+        nc.scalar.activation(log_den[:], den[:], ACT.Ln, bias=0.5)
+        inv = tile([P, PACK, S], F32, "inv")
+        nc.scalar.activation(inv[:], log_den[:], ACT.Exp, scale=-1.0)
+
+        half_y = [tile([P, W], F32, f"half_y{t}") for t in range(PACK)]
+        d_at = [tile([P, W], F32, f"d_at{t}") for t in range(PACK)]
+        m_plain = tile([P, PACK, S], F32, "m_plain")
+        for t in range(PACK):
+            nc.vector.tensor_scalar(half_y[t][:], m_win[t][:].indirect(l1[:]), -0.5, 0.0, ALU.mult, ALU.add)
+            nc.vector.tensor_copy(d_at[t][:], d_win[t][:].indirect(l2[:]))
+        w4 = deal(w4raw, I32, "w4")
+        for t in range(PACK):
+            nc.vector.tensor_tensor(m_win[t][:].indirect(l1[:]), d_at[t][:], half_y[t][:], ALU.add)
+            nc.scalar.copy(m_plain[:, t, :], m_win[t][:, :S])
+        diff = tile([P, PACK, S], F32, "diff")
+        for t in range(PACK):
+            nc.vector.tensor_tensor(diff[:, t, :], m_win[t][:].indirect(l3[:]), m_plain[:, t, :], ALU.subtract)
+
+        h_win = [tile([P, 2 * S], F32, f"h_win{t}") for t in range(PACK)]
+        h_two = [tile([P, S], F32, f"h_two{t}") for t in range(PACK)]
+        z_words = tile([P, S], U32, "z_words")
+        z_scales = tile([P, S], U8, "z_scales")
+        for c, (a, b) in enumerate(Z_CHUNKS):
+            z = tile([P, (b - a) * PACK], BF16, f"z{c}")
+            nc.vector.tensor_tensor(
+                z[:].rearrange("p (c i t) -> p c t i", t=PACK, i=4),
+                diff[:, :, a:b].rearrange("p t (c i) -> p c t i", i=4),
+                inv[:, :, a:b].rearrange("p t (c i) -> p c t i", i=4),
+                ALU.mult,
+            )
+            nc.vector.quantize_mx(out=z_words[:, a:b].bitcast(FP8X4), scales=z_scales[:, a:b], in_=z[:])
+            for t in range(PACK):
+                acc = bank(4 * c + t, b - a)
+                product(acc[:], t, w4, s24, 4, z_words[:, a:b], z_scales[:, a:b])
+                nc.scalar.copy(h_win[t][:, a:b], acc[:])
+                nc.scalar.copy(h_two[t][:, a:b], acc[:])
+
+        top = []
+        for t in range(PACK):
+            six = tile([P, S], F32, f"six{t}")
+            seven = tile([P, S], F32, f"seven{t}")
+            nc.vector.tensor_tensor(six[:], h_win[t][:].indirect(l6[:]), h_two[t][:], ALU.subtract)
+            nc.vector.tensor_tensor(seven[:], h_win[t][:].indirect(l7[:]), h_two[t][:], ALU.subtract)
+            most = tile([P, S], F32, f"most{t}")
+            nc.vector.tensor_tensor(most[:], six[:], seven[:], ALU.max)
+            top.append(most)
+
+        o_words = tile([P, S], I32, "o_words")
+        o_scales = tile([P, S], U8, "o_scales")
+        out_rows = out_0.rearrange("(p t) j -> p t j", t=PACK)
+        out_words = out_1[0].rearrange("p n t -> p (n t)").bitcast(I32)
+        for c, (a, b) in enumerate(OUT_CHUNKS):
+            res = tile([P, PACK, b - a], F32, f"res{c}")
+            for t in range(PACK):
+                nc.vector.tensor_tensor(
+                    res[:, t, :], h_two[t][:].indirect(l5[:, a // 16 : b // 16]), top[t][:, a:b], ALU.subtract
+                )
+            nc.sync.dma_start(out_rows[:, :, a:b], res[:])
+            rounded = tile([P, (b - a) * PACK], BF16, f"rounded{c}")
+            dst = rounded[:].rearrange("p (c i t) -> p c t i", t=PACK, i=4)
+            src = res[:].rearrange("p t (c i) -> p c t i", i=4)
+            if c == len(OUT_CHUNKS) - 1:
+                nc.vector.tensor_copy(dst, src)
+            else:
+                nc.scalar.copy(dst, src)
+            nc.vector.quantize_mx(out=o_words[:, a:b].bitcast(FP8X4), scales=o_scales[:, a:b], in_=rounded[:])
+            nc.sync.dma_start(out_words[:, a:b], o_words[:, a:b])
+        for q in range(4):
+            queue = nc.scalar if q % 2 == 0 else nc.sync
+            queue.dma_start(
+                out_2[0, 4 * q : 4 * q + 4, :].bitcast(I32), o_scales[32 * q : 32 * q + 4, :].bitcast(I32)
+            )

@@ -1,6 +1,7 @@
 from contextlib import ExitStack
 
 import concourse.mybir as mybir
+from concourse.masks import make_identity
 
 K, T, S, H, N, W = 512, 2048, 512, 512, 512, 256
 P = 128
@@ -17,8 +18,9 @@ FP8X4 = mybir.dt.float8_e4m3fn_x4
 ALU = mybir.AluOpType
 ACT = mybir.ActivationFunctionType
 
-Z_CHUNKS = ((0, 256), (256, 512))
+Z_CHUNKS = ((0, 256), (256, 384), (384, 512))
 OUT_CHUNKS = ((0, 256), (256, 384), (384, 512))
+ON_SCALAR = 3
 
 
 def tile_picked_trioputbnormbtrim_none_po_kernel(
@@ -29,10 +31,14 @@ def tile_picked_trioputbnormbtrim_none_po_kernel(
     with ExitStack() as ctx:
         lists = ctx.enter_context(tc.tile_pool(name="lists", bufs=1))
         sb = ctx.enter_context(tc.tile_pool(name="sb", bufs=1))
+        shared = ctx.enter_context(tc.tile_pool(name="shared", bufs=1))
         psum = ctx.enter_context(tc.psum_pool(name="psum", bufs=1))
 
-        def tile(shape, dtype, name):
-            return sb.tile(shape, dtype, name=name, align_bytes=64)
+        def tile(shape, dtype, name, slot=None):
+            return sb.tile(shape, dtype, name=name, tag=slot or name, align_bytes=64)
+
+        def placed(shape, dtype, name, offset):
+            return shared.tile(shape, dtype, name=name, align_bytes=64, offset=offset)
 
         def bank(index, width):
             return psum.tile([P, width], F32, name=f"bank{index}")
@@ -42,10 +48,8 @@ def tile_picked_trioputbnormbtrim_none_po_kernel(
             nc.sync.dma_start(dst[:], src)
             return dst
 
-        def load_words(src, name):
-            dst = tile([P, src.shape[2]], I32, name)
+        def load_words(dst, src):
             nc.sync.dma_start(dst[:], src[0].rearrange("p n t -> p (n t)").bitcast(I32))
-            return dst
 
         def load_scales(queue, dst, first, src):
             for q in range(4):
@@ -54,36 +58,45 @@ def tile_picked_trioputbnormbtrim_none_po_kernel(
                     src[0, 4 * q : 4 * q + 4, :].bitcast(I32),
                 )
 
+        xw = tile([P, T], I32, "xw")
         xs = tile([P, T], U8, "xs")
-        ws31 = tile([P, H], U8, "ws31")
-        ws24 = tile([P, H], U8, "ws24")
-        nc.vector.memset(xs[:].bitcast(I32), 0)
-        nc.vector.memset(ws31[:].bitcast(I32), 0)
-        nc.gpsimd.memset(ws24[:].bitcast(I32), 0)
-
-        xw = load_words(x_words, "xw")
-        l_three = load_list(three, "three")
-        load_scales(nc.scalar, xs, 0, x_scales)
-        l_offs = load_list(offs, "offs")
-        w3raw = load_words(w3_words, "w3raw")
-        load_scales(nc.sync, ws31, 0, w3_scales)
-        load_scales(nc.sync, ws31, 4, w1_scales)
-        load_scales(nc.gpsimd, ws24, 4, w4_scales)
+        w3raw = placed([P, H], I32, "w3raw", 0)
+        ws3 = placed([P, H], U8, "ws3", 2048)
+        w1raw = placed([P, H], I32, "w1raw", 4096)
+        ws124 = placed([P, H], U8, "ws124", 6144)
+        w2raw = tile([P, H], I32, "w2raw")
+        w4raw = tile([P, H], I32, "w4raw")
         gain = tile([P, PACK], F32, "gain")
-        nc.gpsimd.dma_start(gain[:], gn.rearrange("(p t) o -> p (t o)", t=PACK))
-        w1raw = load_words(w1_words, "w1raw")
+        nc.gpsimd.memset(xs[:].bitcast(I32), 0)
+        nc.vector.memset(ws3[:].bitcast(I32), 0)
+        nc.vector.memset(ws124[:].bitcast(I32), 0)
+        warm = tile([P, 2], F32, "warm")
+        nc.vector.memset(warm[:, 0:1], 1.0)
+        nc.scalar.activation(warm[:, 1:2], warm[:, 0:1], ACT.Ln)
+
+        l_three = load_list(three, "three")
+        l_offs = load_list(offs, "offs")
+        load_words(xw, x_words)
+        load_scales(nc.sync, xs, 0, x_scales)
+        load_words(w3raw, w3_words)
+        load_scales(nc.sync, ws3, 0, w3_scales)
         l_two = load_list(two, "two")
+        nc.gpsimd.dma_start(gain[:], gn.rearrange("(p t) o -> p (t o)", t=PACK))
+        load_scales(nc.gpsimd, ws124, 8, w4_scales)
+        load_words(w1raw, w1_words)
+        load_scales(nc.sync, ws124, 0, w1_scales)
+        load_scales(nc.sync, ws124, 4, w2_scales)
+        load_words(w2raw, w2_words)
         l4 = load_list(n4, "n4")
-        load_scales(nc.sync, ws24, 0, w2_scales)
-        w2raw = load_words(w2_words, "w2raw")
         l1 = load_list(n1, "n1")
         l2 = load_list(n2, "n2")
+        load_words(w4raw, w4_words)
         l3 = load_list(n3, "n3")
-        w4raw = load_words(w4_words, "w4raw")
         l6 = load_list(n6, "n6")
         l7 = load_list(n7, "n7")
         l5 = load_list(n5, "n5")
-
+        ident = tile([P, P], F32, "ident")
+        make_identity(nc, ident[:])
         neg_gain = tile([P, PACK], F32, "neg_gain")
         nc.gpsimd.tensor_scalar(neg_gain[:], gain[:], -1.0, 0.0, ALU.mult, ALU.add)
 
@@ -95,15 +108,9 @@ def tile_picked_trioputbnormbtrim_none_po_kernel(
             )
             return dealt
 
-        def pick_words(lst, name):
-            dst = tile([P, S], U32, name)
-            nc.vector.tensor_copy(dst[:], xw[:].bitcast(U32).indirect(lst[:]))
-            return dst
-
-        def pick_scales(lst, name):
-            dst = tile([P, S], U8, name)
-            nc.vector.tensor_copy(dst[:], xs[:].indirect(lst[:]))
-            return dst
+        def pick(words, scale, lst):
+            nc.vector.tensor_copy(words[:], xw[:].bitcast(U32).indirect(lst[:]))
+            nc.vector.tensor_copy(scale[:], xs[:].indirect(lst[:]))
 
         def product(acc, t, w, w_scale, first, words, scale):
             cols = slice(P * t, P * (t + 1))
@@ -112,56 +119,80 @@ def tile_picked_trioputbnormbtrim_none_po_kernel(
                 rhs=words.bitcast(FP8X4), rhs_scale=scale, start=True, stop=True,
             )
 
-        x3w = pick_words(l_three, "x3w")
-        x3s = pick_scales(l_three, "x3s")
+        x3w, x3s = tile([P, S], U32, "x3w"), tile([P, S], U8, "x3s")
+        pick(x3w, x3s, l_three)
         w3 = deal(w3raw, I32, "w3")
-        s31 = deal(ws31, U8, "s31")
-        x1w = pick_words(l_offs, "x1w")
-        x1s = pick_scales(l_offs, "x1s")
+        s3 = deal(ws3, U8, "s3")
+        x1w, x1s = placed([P, S], U32, "x1w", 256), placed([P, S], U8, "x1s", 2304)
+        pick(x1w, x1s, l_offs)
         w1 = deal(w1raw, I32, "w1")
-        x2w = pick_words(l_two, "x2w")
-        x2s = pick_scales(l_two, "x2s")
+        s124 = deal(ws124, U8, "s124")
+        x2w, x2s = placed([P, S], U32, "x2w", 4352), placed([P, S], U8, "x2s", 6400)
+        pick(x2w, x2s, l_two)
         w2 = deal(w2raw, I32, "w2")
-        s24 = deal(ws24, U8, "s24")
 
         size_win = [tile([P, 2 * S], F32, f"size_win{t}") for t in range(PACK)]
         size = tile([P, PACK, S], F32, "size")
-        for t in range(PACK):
+        for t in reversed(range(PACK)):
             acc = bank(t, S)
-            product(acc[:], t, w3, s31, 0, x3w[:], x3s[:])
-            nc.scalar.activation(size_win[t][:, :S], acc[:], ACT.Abs)
+            product(acc[:], t, w3, s3, 0, x3w[:], x3s[:])
             nc.scalar.activation(size[:, t, :], acc[:], ACT.Abs)
+            if t >= ON_SCALAR:
+                nc.scalar.activation(size_win[t][:, :S], acc[:], ACT.Abs)
 
         m_win = [tile([P, 2 * S], F32, f"m_win{t}") for t in range(PACK)]
         for t in range(PACK):
             acc = bank(4 + t, S)
-            product(acc[:], t, w1, s31, 4, x1w[:], x1s[:])
+            product(acc[:], t, w1, s124, 0, x1w[:], x1s[:])
             nc.scalar.activation(m_win[t][:, :S], acc[:], ACT.Copy, scale=neg_gain[:, t : t + 1])
 
         d_win = [tile([P, S], F32, f"d_win{t}") for t in range(PACK)]
         for t in range(PACK):
             acc = bank(t, S)
-            product(acc[:], t, w2, s24, 0, x2w[:], x2s[:])
+            product(acc[:], t, w2, s124, 4, x2w[:], x2s[:])
             nc.scalar.activation(d_win[t][:], acc[:], ACT.Copy, scale=neg_gain[:, t : t + 1])
 
-        den = tile([P, PACK, S], F32, "den")
-        for t in range(PACK):
-            nc.vector.tensor_tensor(den[:, t, :], size_win[t][:].indirect(l4[:]), size[:, t, :], ALU.add)
-        log_den = tile([P, PACK, S], F32, "log_den")
-        nc.scalar.activation(log_den[:], den[:], ACT.Ln, bias=0.5)
+        logs = [tile([P, S], F32, f"logs{t}") for t in range(PACK)]
         inv = tile([P, PACK, S], F32, "inv")
-        nc.scalar.activation(inv[:], log_den[:], ACT.Exp, scale=-1.0)
+        for t in range(ON_SCALAR):
+            nc.scalar.activation(size_win[t][:, :S], size[:, t, :], ACT.Ln, bias=0.25)
+        for t in range(ON_SCALAR, PACK):
+            both = tile([P, S], F32, f"both{t}")
+            nc.vector.tensor_tensor(both[:], size_win[t][:].indirect(l4[:]), size[:, t, :], ALU.add)
+            nc.scalar.activation(logs[t][:], both[:], ACT.Ln, bias=0.5)
 
-        half_y = [tile([P, W], F32, f"half_y{t}") for t in range(PACK)]
-        d_at = [tile([P, W], F32, f"d_at{t}") for t in range(PACK)]
+        far = tile([P, ON_SCALAR, S], F32, "far", "w2")
+        for t in range(ON_SCALAR):
+            nc.scalar.activation(far[:, t, :], size_win[t][:].indirect(l4[:]), ACT.Exp)
+        for t in range(ON_SCALAR, PACK):
+            nc.scalar.activation(inv[:, t, :], logs[t][:], ACT.Exp, scale=-1.0)
+        for t in range(ON_SCALAR):
+            acc = bank(4 + t, S)
+            for c in range(4):
+                cols = slice(P * c, P * (c + 1))
+                nc.tensor.matmul(acc[:, cols], size[:, t, cols], ident[:], start=True, stop=False, is_transpose=True)
+                nc.tensor.matmul(acc[:, cols], far[:, t, cols], ident[:], start=False, stop=True, is_transpose=True)
+            nc.scalar.activation(logs[t][:], acc[:], ACT.Ln, bias=0.25)
+        for c in range(4):
+            cols = slice(P * c, P * (c + 1))
+            acc = bank(c, ON_SCALAR * P)
+            for t in range(ON_SCALAR):
+                nc.tensor.transpose(acc[:, P * t : P * (t + 1)], logs[t][:, cols], ident[:])
+            nc.scalar.activation(
+                inv[:, :ON_SCALAR, cols], acc[:].rearrange("p (t j) -> p t j", j=P), ACT.Exp, scale=-1.0
+            )
+
+        half_y = tile([P, PACK, W], F32, "half_y")
+        d_at = tile([P, PACK, W], F32, "d_at", "neg_gain")
         m_plain = tile([P, PACK, S], F32, "m_plain")
         for t in range(PACK):
-            nc.vector.tensor_scalar(half_y[t][:], m_win[t][:].indirect(l1[:]), -0.5, 0.0, ALU.mult, ALU.add)
-            nc.vector.tensor_copy(d_at[t][:], d_win[t][:].indirect(l2[:]))
+            nc.vector.tensor_scalar(half_y[:, t, :], m_win[t][:].indirect(l1[:]), -0.5, 0.0, ALU.mult, ALU.add)
         w4 = deal(w4raw, I32, "w4")
         for t in range(PACK):
-            nc.vector.tensor_tensor(m_win[t][:].indirect(l1[:]), d_at[t][:], half_y[t][:], ALU.add)
-            nc.scalar.copy(m_plain[:, t, :], m_win[t][:, :S])
+            nc.vector.tensor_copy(d_at[:, t, :], d_win[t][:].indirect(l2[:]))
+        for t in range(PACK):
+            nc.vector.tensor_tensor(m_win[t][:].indirect(l1[:]), d_at[:, t, :], half_y[:, t, :], ALU.add)
+            nc.sync.dma_start(m_plain[:, t, :], m_win[t][:, :S])
         diff = tile([P, PACK, S], F32, "diff")
         for t in range(PACK):
             nc.vector.tensor_tensor(diff[:, t, :], m_win[t][:].indirect(l3[:]), m_plain[:, t, :], ALU.subtract)
@@ -179,9 +210,10 @@ def tile_picked_trioputbnormbtrim_none_po_kernel(
                 ALU.mult,
             )
             nc.vector.quantize_mx(out=z_words[:, a:b].bitcast(FP8X4), scales=z_scales[:, a:b], in_=z[:])
-            for t in range(PACK):
-                acc = bank(4 * c + t, b - a)
-                product(acc[:], t, w4, s24, 4, z_words[:, a:b], z_scales[:, a:b])
+        for t in range(PACK):
+            for c, (a, b) in enumerate(Z_CHUNKS):
+                acc = bank(4 * (c % 2) + t, b - a)
+                product(acc[:], t, w4, s124, 8, z_words[:, a:b], z_scales[:, a:b])
                 nc.scalar.copy(h_win[t][:, a:b], acc[:])
                 nc.scalar.copy(h_two[t][:, a:b], acc[:])
 

from contextlib import ExitStack

import concourse.mybir as mybir
from concourse.masks import make_identity

K, T, S, H, N, W = 512, 2048, 512, 512, 512, 256
P = 128
PACK = 4
FLOPS = 4 * 2 * K * H * S

F32 = mybir.dt.float32
BF16 = mybir.dt.bfloat16
I32 = mybir.dt.int32
U32 = mybir.dt.uint32
U16 = mybir.dt.uint16
U8 = mybir.dt.uint8
FP8X4 = mybir.dt.float8_e4m3fn_x4
ALU = mybir.AluOpType
ACT = mybir.ActivationFunctionType

Z_CHUNKS = ((0, 256), (256, 384), (384, 512))
OUT_CHUNKS = ((0, 256), (256, 384), (384, 512))
ON_SCALAR = 3


def tile_picked_trioputbnormbtrim_none_po_kernel(
    tc, x_words, x_scales, w1_words, w1_scales, w2_words, w2_scales, w3_words, w3_scales, gn,
    w4_words, w4_scales, offs, two, three, n1, n2, n3, n4, n5, n6, n7, out_0, out_1, out_2,
):
    nc = tc.nc
    with ExitStack() as ctx:
        lists = ctx.enter_context(tc.tile_pool(name="lists", bufs=1))
        sb = ctx.enter_context(tc.tile_pool(name="sb", bufs=1))
        shared = ctx.enter_context(tc.tile_pool(name="shared", bufs=1))
        psum = ctx.enter_context(tc.psum_pool(name="psum", bufs=1))

        def tile(shape, dtype, name, slot=None):
            return sb.tile(shape, dtype, name=name, tag=slot or name, align_bytes=64)

        def placed(shape, dtype, name, offset):
            return shared.tile(shape, dtype, name=name, align_bytes=64, offset=offset)

        def bank(index, width):
            return psum.tile([P, width], F32, name=f"bank{index}")

        def load_list(src, name):
            dst = lists.tile(list(src.shape), U16, name=name)
            nc.sync.dma_start(dst[:], src)
            return dst

        def load_words(dst, src):
            nc.sync.dma_start(dst[:], src[0].rearrange("p n t -> p (n t)").bitcast(I32))

        def load_scales(queue, dst, first, src):
            for q in range(4):
                queue.dma_start(
                    dst[32 * q + first : 32 * q + first + 4, :].bitcast(I32),
                    src[0, 4 * q : 4 * q + 4, :].bitcast(I32),
                )

        xw = tile([P, T], I32, "xw")
        xs = tile([P, T], U8, "xs")
        w3raw = placed([P, H], I32, "w3raw", 0)
        ws3 = placed([P, H], U8, "ws3", 2048)
        w1raw = placed([P, H], I32, "w1raw", 4096)
        ws124 = placed([P, H], U8, "ws124", 6144)
        w2raw = tile([P, H], I32, "w2raw")
        w4raw = tile([P, H], I32, "w4raw")
        gain = tile([P, PACK], F32, "gain")
        nc.gpsimd.memset(xs[:].bitcast(I32), 0)
        nc.vector.memset(ws3[:].bitcast(I32), 0)
        nc.vector.memset(ws124[:].bitcast(I32), 0)
        warm = tile([P, 2], F32, "warm")
        nc.vector.memset(warm[:, 0:1], 1.0)
        nc.scalar.activation(warm[:, 1:2], warm[:, 0:1], ACT.Ln)

        l_three = load_list(three, "three")
        l_offs = load_list(offs, "offs")
        load_words(xw, x_words)
        load_scales(nc.sync, xs, 0, x_scales)
        load_words(w3raw, w3_words)
        load_scales(nc.sync, ws3, 0, w3_scales)
        l_two = load_list(two, "two")
        nc.gpsimd.dma_start(gain[:], gn.rearrange("(p t) o -> p (t o)", t=PACK))
        load_scales(nc.gpsimd, ws124, 8, w4_scales)
        load_words(w1raw, w1_words)
        load_scales(nc.sync, ws124, 0, w1_scales)
        load_scales(nc.sync, ws124, 4, w2_scales)
        load_words(w2raw, w2_words)
        l4 = load_list(n4, "n4")
        l1 = load_list(n1, "n1")
        l2 = load_list(n2, "n2")
        load_words(w4raw, w4_words)
        l3 = load_list(n3, "n3")
        l6 = load_list(n6, "n6")
        l7 = load_list(n7, "n7")
        l5 = load_list(n5, "n5")
        ident = tile([P, P], F32, "ident")
        make_identity(nc, ident[:])
        neg_gain = tile([P, PACK], F32, "neg_gain")
        nc.gpsimd.tensor_scalar(neg_gain[:], gain[:], -1.0, 0.0, ALU.mult, ALU.add)

        def deal(raw, dtype, name):
            dealt = tile([P, H], dtype, name)
            nc.vector.tensor_copy(
                dealt[:].rearrange("p (t c i) -> p c t i", t=PACK, i=4),
                raw[:].rearrange("p (c i t) -> p c t i", t=PACK, i=4),
            )
            return dealt

        def pick(words, scale, lst):
            nc.vector.tensor_copy(words[:], xw[:].bitcast(U32).indirect(lst[:]))
            nc.vector.tensor_copy(scale[:], xs[:].indirect(lst[:]))

        def product(acc, t, w, w_scale, first, words, scale):
            cols = slice(P * t, P * (t + 1))
            nc.tensor.matmul_mx(
                out=acc, lhsT=w[:, cols].bitcast(FP8X4), lhsT_scale=w_scale[first:P, cols],
                rhs=words.bitcast(FP8X4), rhs_scale=scale, start=True, stop=True,
            )

        x3w, x3s = tile([P, S], U32, "x3w"), tile([P, S], U8, "x3s")
        pick(x3w, x3s, l_three)
        w3 = deal(w3raw, I32, "w3")
        s3 = deal(ws3, U8, "s3")
        x1w, x1s = placed([P, S], U32, "x1w", 256), placed([P, S], U8, "x1s", 2304)
        pick(x1w, x1s, l_offs)
        w1 = deal(w1raw, I32, "w1")
        s124 = deal(ws124, U8, "s124")
        x2w, x2s = placed([P, S], U32, "x2w", 4352), placed([P, S], U8, "x2s", 6400)
        pick(x2w, x2s, l_two)
        w2 = deal(w2raw, I32, "w2")

        size_win = [tile([P, 2 * S], F32, f"size_win{t}") for t in range(PACK)]
        size = tile([P, PACK, S], F32, "size")
        for t in reversed(range(PACK)):
            acc = bank(t, S)
            product(acc[:], t, w3, s3, 0, x3w[:], x3s[:])
            nc.scalar.activation(size[:, t, :], acc[:], ACT.Abs)
            if t >= ON_SCALAR:
                nc.scalar.activation(size_win[t][:, :S], acc[:], ACT.Abs)

        m_win = [tile([P, 2 * S], F32, f"m_win{t}") for t in range(PACK)]
        for t in range(PACK):
            acc = bank(4 + t, S)
            product(acc[:], t, w1, s124, 0, x1w[:], x1s[:])
            nc.scalar.activation(m_win[t][:, :S], acc[:], ACT.Copy, scale=neg_gain[:, t : t + 1])

        d_win = [tile([P, S], F32, f"d_win{t}") for t in range(PACK)]
        for t in range(PACK):
            acc = bank(t, S)
            product(acc[:], t, w2, s124, 4, x2w[:], x2s[:])
            nc.scalar.activation(d_win[t][:], acc[:], ACT.Copy, scale=neg_gain[:, t : t + 1])

        logs = [tile([P, S], F32, f"logs{t}") for t in range(PACK)]
        inv = tile([P, PACK, S], F32, "inv")
        for t in range(ON_SCALAR):
            nc.scalar.activation(size_win[t][:, :S], size[:, t, :], ACT.Ln, bias=0.25)
        for t in range(ON_SCALAR, PACK):
            both = tile([P, S], F32, f"both{t}")
            nc.vector.tensor_tensor(both[:], size_win[t][:].indirect(l4[:]), size[:, t, :], ALU.add)
            nc.scalar.activation(logs[t][:], both[:], ACT.Ln, bias=0.5)

        far = tile([P, ON_SCALAR, S], F32, "far", "w2")
        for t in range(ON_SCALAR):
            nc.scalar.activation(far[:, t, :], size_win[t][:].indirect(l4[:]), ACT.Exp)
        for t in range(ON_SCALAR, PACK):
            nc.scalar.activation(inv[:, t, :], logs[t][:], ACT.Exp, scale=-1.0)
        for t in range(ON_SCALAR):
            acc = bank(4 + t, S)
            for c in range(4):
                cols = slice(P * c, P * (c + 1))
                nc.tensor.matmul(acc[:, cols], size[:, t, cols], ident[:], start=True, stop=False, is_transpose=True)
                nc.tensor.matmul(acc[:, cols], far[:, t, cols], ident[:], start=False, stop=True, is_transpose=True)
            nc.scalar.activation(logs[t][:], acc[:], ACT.Ln, bias=0.25)
        for c in range(4):
            cols = slice(P * c, P * (c + 1))
            acc = bank(c, ON_SCALAR * P)
            for t in range(ON_SCALAR):
                nc.tensor.transpose(acc[:, P * t : P * (t + 1)], logs[t][:, cols], ident[:])
            nc.scalar.activation(
                inv[:, :ON_SCALAR, cols], acc[:].rearrange("p (t j) -> p t j", j=P), ACT.Exp, scale=-1.0
            )

        half_y = tile([P, PACK, W], F32, "half_y")
        d_at = tile([P, PACK, W], F32, "d_at", "neg_gain")
        m_plain = tile([P, PACK, S], F32, "m_plain")
        for t in range(PACK):
            nc.vector.tensor_scalar(half_y[:, t, :], m_win[t][:].indirect(l1[:]), -0.5, 0.0, ALU.mult, ALU.add)
        w4 = deal(w4raw, I32, "w4")
        for t in range(PACK):
            nc.vector.tensor_copy(d_at[:, t, :], d_win[t][:].indirect(l2[:]))
        for t in range(PACK):
            nc.vector.tensor_tensor(m_win[t][:].indirect(l1[:]), d_at[:, t, :], half_y[:, t, :], ALU.add)
            nc.sync.dma_start(m_plain[:, t, :], m_win[t][:, :S])
        diff = tile([P, PACK, S], F32, "diff")
        for t in range(PACK):
            nc.vector.tensor_tensor(diff[:, t, :], m_win[t][:].indirect(l3[:]), m_plain[:, t, :], ALU.subtract)

        h_win = [tile([P, 2 * S], F32, f"h_win{t}") for t in range(PACK)]
        h_two = [tile([P, S], F32, f"h_two{t}") for t in range(PACK)]
        z_words = tile([P, S], U32, "z_words")
        z_scales = tile([P, S], U8, "z_scales")
        for c, (a, b) in enumerate(Z_CHUNKS):
            z = tile([P, (b - a) * PACK], BF16, f"z{c}")
            nc.vector.tensor_tensor(
                z[:].rearrange("p (c i t) -> p c t i", t=PACK, i=4),
                diff[:, :, a:b].rearrange("p t (c i) -> p c t i", i=4),
                inv[:, :, a:b].rearrange("p t (c i) -> p c t i", i=4),
                ALU.mult,
            )
            nc.vector.quantize_mx(out=z_words[:, a:b].bitcast(FP8X4), scales=z_scales[:, a:b], in_=z[:])
        for t in range(PACK):
            for c, (a, b) in enumerate(Z_CHUNKS):
                acc = bank(4 * (c % 2) + t, b - a)
                product(acc[:], t, w4, s124, 8, z_words[:, a:b], z_scales[:, a:b])
                nc.scalar.copy(h_win[t][:, a:b], acc[:])
                nc.scalar.copy(h_two[t][:, a:b], acc[:])

        top = []
        for t in range(PACK):
            six = tile([P, S], F32, f"six{t}")
            seven = tile([P, S], F32, f"seven{t}")
            nc.vector.tensor_tensor(six[:], h_win[t][:].indirect(l6[:]), h_two[t][:], ALU.subtract)
            nc.vector.tensor_tensor(seven[:], h_win[t][:].indirect(l7[:]), h_two[t][:], ALU.subtract)
            most = tile([P, S], F32, f"most{t}")
            nc.vector.tensor_tensor(most[:], six[:], seven[:], ALU.max)
            top.append(most)

        o_words = tile([P, S], I32, "o_words")
        o_scales = tile([P, S], U8, "o_scales")
        out_rows = out_0.rearrange("(p t) j -> p t j", t=PACK)
        out_words = out_1[0].rearrange("p n t -> p (n t)").bitcast(I32)
        for c, (a, b) in enumerate(OUT_CHUNKS):
            res = tile([P, PACK, b - a], F32, f"res{c}")
            for t in range(PACK):
                nc.vector.tensor_tensor(
                    res[:, t, :], h_two[t][:].indirect(l5[:, a // 16 : b // 16]), top[t][:, a:b], ALU.subtract
                )
            nc.sync.dma_start(out_rows[:, :, a:b], res[:])
            rounded = tile([P, (b - a) * PACK], BF16, f"rounded{c}")
            dst = rounded[:].rearrange("p (c i t) -> p c t i", t=PACK, i=4)
            src = res[:].rearrange("p t (c i) -> p c t i", i=4)
            if c == len(OUT_CHUNKS) - 1:
                nc.vector.tensor_copy(dst, src)
            else:
                nc.scalar.copy(dst, src)
            nc.vector.quantize_mx(out=o_words[:, a:b].bitcast(FP8X4), scales=o_scales[:, a:b], in_=rounded[:])
            nc.sync.dma_start(out_words[:, a:b], o_words[:, a:b])
        for q in range(4):
            queue = nc.scalar if q % 2 == 0 else nc.sync
            queue.dma_start(
                out_2[0, 4 * q : 4 * q + 4, :].bitcast(I32), o_scales[32 * q : 32 * q + 4, :].bitcast(I32)
            )
